import numpy as np
CORES = [10,14,66,70,74,78,82,86,90,94,106,110]
N = 12
W = 128
def setup_inputs(rng):
    amp = 0.5 + 1.5 * rng.random((2, N, 128, 1), dtype=np.float32)
    return {"u": amp[0] * rng.standard_normal((N, 128, W), dtype=np.float32), "b": amp[1] * rng.standard_normal((N, 128, W), dtype=np.float32)}
def setup_inputs_big(rng):
    d = setup_inputs(rng)
    for k in ("u", "b"): d[k] = (d[k].astype(np.float32) * 1024.0).astype(d[k].dtype)
    return d
def setup_inputs_small(rng):
    d = setup_inputs(rng)
    for k in ("u", "b"): d[k] = (d[k].astype(np.float32) * (1 / 1024.0)).astype(d[k].dtype)
    return d
def setup_inputs_apart(rng):
    d = setup_inputs(rng)
    f = (10.0 ** rng.permutation(np.linspace(-1.5, 1.5, N))).astype(np.float32).reshape(N, 1, 1)
    for k in ("u", "b"): d[k] = (d[k].astype(np.float32) * f).astype(d[k].dtype)
    return d
def reference(u, b):
    g = np.concatenate(list(u.astype(np.float64)), axis=1); bb = np.concatenate(list(b.astype(np.float64)), axis=1)
    p = np.concatenate([g[:, -2:], g, g[:, :2]], axis=1)
    n = 0.125 * (p[:, :-4] + p[:, 1:-3] + p[:, 3:-1] + p[:, 4:]) + 0.5 * bb
    d = n - g
    s = np.stack([(d ** 2).mean(axis=1), np.abs(d).max(axis=1)], axis=1)
    return {"y": np.stack([n[:, W * r:W * r + W] for r in range(N)]).astype(np.float32), "s": np.broadcast_to(s.astype(np.float32), (N, 128, 2))}

@@ -1,0 +1,185 @@
+from concourse.bass import DstId, RemoteDMATransfer
+from concourse.mybir import AluOpType
+
+N = 12
+F32 = "float32"
+SCRATCH = {
+    "ue": ("sbuf", [128, 136], F32), "bb": ("sbuf", [128, 128], F32),
+    "c125": ("sbuf", [128, 132], F32), "c5": ("sbuf", [128, 128], F32),
+    "pp": ("sbuf", [128, 136], F32), "a8": ("sbuf", [128, 132], F32), "dd": ("sbuf", [128, 132], F32),
+    "yb": ("sbuf", [128, 128], F32), "hin": ("sbuf", [128, 4], F32), "t4": ("sbuf", [128, 4], F32),
+    "sqa": ("sbuf", [128, 64], F32), "aba": ("sbuf", [128, 64], F32),
+    "land": ("sbuf", [128, 13, 12], F32),
+    "dB": ("sbuf", [128, 12, 4], F32), "nB": ("sbuf", [128, 12, 4], F32), "zt": ("sbuf", [128, 12, 4], F32),
+    "r6s": ("sbuf", [128, 6, 5], F32), "r6m": ("sbuf", [128, 6, 5], F32),
+    "r3s": ("sbuf", [128, 3, 5], F32), "r3m": ("sbuf", [128, 3, 5], F32),
+    "t5s": ("sbuf", [128, 8], F32), "t5m": ("sbuf", [128, 8], F32),
+    "t2s": ("sbuf", [128, 4], F32), "t2m": ("sbuf", [128, 4], F32),
+    "sc": ("sbuf", [128, 4], F32), "so": ("sbuf", [128, 2], F32),
+    "Ap": ("psum", [128, 512], F32), "hbp": ("psum", [128, 512], F32), "nwp": ("psum", [128, 512], F32),
+    "ndp": ("psum", [128, 512], F32), "sqb": ("psum", [128, 512], F32), "abb": ("psum", [128, 512], F32),
+}
+SEMAPHORES = ["ldu", "ldb", "v", "mr", "halo", "arr", "sent", "yr", "sr", "sty", "sts"]
+
+
+def _bits(m):
+    return bin(m).count("1")
+
+
+def rank_program(g, core, T, topo):
+    rank = T.rank_of(core)
+    if rank is None:
+        return
+    cores = list(T.cores)
+    S = T.sem
+    v = g.vector
+    ADD, SUB, MUL, MAX = AluOpType.add, AluOpType.subtract, AluOpType.mult, AluOpType.max
+
+    def emask(src, dst):
+        m = topo.mask(src, dst)
+        if topo.chip(src) != topo.chip(dst):
+            return m
+        off = 0
+        for c in cores:
+            if topo.chip(c) != topo.chip(src):
+                off |= topo.mask(src, c)
+        return (m & ~off) or m
+
+    def hops(src, dst):
+        a, b = topo.chip(src), topo.chip(dst)
+        if a == b:
+            return 0
+        return 1 if (topo.mates(a, b) or topo.same_plane(a, b)) else 2
+
+    def did(c):
+        rid, pid, _se = topo.addr(c)
+        return DstId(rid=rid, pnc=pid)
+
+    left, right = cores[(rank - 1) % N], cores[(rank + 1) % N]
+    others = sorted([c for c in cores if c != core], key=lambda c: -hops(core, c))
+
+    g.sync.dma_start(T.ue[:, 4:132], T.u[:, :]).then_inc(S.ldu, 16)
+    g.scalar.dma_start(T.bb[:, :], T.b[:, :]).then_inc(S.ldb, 16)
+
+    g.wait_ge(S.ldu, 16)
+    g.remote_dma_fused([
+        RemoteDMATransfer(dst_ids=[did(left)], dma_engine_mask=emask(core, left), remote_sem=S.halo,
+                          srcs=[T.ue[:, 4:6]], dsts=[T.hin[:, 2:4]], alu_op=0),
+        RemoteDMATransfer(dst_ids=[did(right)], dma_engine_mask=emask(core, right), remote_sem=S.halo,
+                          srcs=[T.ue[:, 130:132]], dsts=[T.hin[:, 0:2]], alu_op=0),
+    ], local_sem=S.sent)
+    n_sent = _bits(emask(core, left)) + _bits(emask(core, right))
+    groups = {}
+    for c in others:
+        groups.setdefault(emask(core, c), []).append(c)
+    g.wait_ge(S.mr, 2)
+    g.remote_dma_fused([
+        RemoteDMATransfer(dst_ids=[did(c) for c in cs], dma_engine_mask=m, remote_sem=S.arr,
+                          srcs=[T.land[:, 0, 0:10]],
+                          dsts=[T.land[:, (rank - T.rank_of(c)) % N, 0:10] for c in cs], alu_op=0)
+        for m, cs in groups.items()], local_sem=S.sent)
+    n_sent += sum(_bits(m) for m in groups)
+    g.wait_ge(S.sent, n_sent)
+    n_halo = _bits(emask(left, core)) + _bits(emask(right, core))
+    n_arr = sum(_bits(emask(c, core)) for c in others)
+
+    cnt = [0]
+
+    def op(ins):
+        ins.then_inc(S.v, 1)
+        cnt[0] += 1
+
+    def bar():
+        v.wait_ge(S.v, cnt[0])
+
+    def tt(out, a, b, o):
+        op(v.tensor_tensor(out, a, b, o))
+
+    op(v.memset(T.ue[:, 0:4], 0.0))
+    op(v.memset(T.ue[:, 132:136], 0.0))
+    op(v.memset(T.c125[:, :], 0.125))
+    op(v.memset(T.c5[:, :], 0.5))
+    op(v.memset(T.hbp[:, 0:2], 0.0))
+    op(v.memset(T.hbp[:, 130:132], 0.0))
+    op(v.memset(T.zt[:, :, :], 0.0))
+    op(v.memset(T.sc[:, :], -1.0 / (N * 128)))
+    bar()
+    v.wait_ge(S.ldu, 16)
+    tt(T.pp[:, 0:135], T.ue[:, 0:135], T.ue[:, 1:136], ADD)
+    bar()
+    tt(T.Ap[:, 0:132], T.pp[:, 0:132], T.pp[:, 3:135], ADD)
+    v.wait_ge(S.ldb, 16)
+    tt(T.hbp[:, 2:130], T.bb[:, :], T.c5[:, :], MUL)
+    bar()
+    tt(T.a8[:, :], T.Ap[:, 0:132], T.c125[:, :], MUL)
+    tt(T.nwp[:, 0:132], T.ue[:, 2:134], T.hbp[:, 0:132], SUB)
+    bar()
+    tt(T.dd[:, 2:130], T.a8[:, 2:130], T.nwp[:, 2:130], SUB)
+    tt(T.ndp[:, 0:124], T.nwp[:, 4:128], T.a8[:, 4:128], SUB)
+    tt(T.land[:, 0, 1:5], T.a8[:, 0:4], T.nwp[:, 0:4], SUB)
+    tt(T.land[:, 0, 5:9], T.a8[:, 128:132], T.nwp[:, 128:132], SUB)
+    bar()
+    tt(T.sqa[:, 0:62], T.dd[:, 4:66], T.ndp[:, 0:62], MUL)
+    tt(T.sqb[:, 0:62], T.dd[:, 66:128], T.ndp[:, 62:124], MUL)
+    tt(T.aba[:, 0:62], T.dd[:, 4:66], T.ndp[:, 0:62], MAX)
+    tt(T.abb[:, 0:62], T.dd[:, 66:128], T.ndp[:, 62:124], MAX)
+    bar()
+    tt(T.sqa[:, 0:62], T.sqa[:, 0:62], T.sqb[:, 0:62], ADD)
+    tt(T.aba[:, 0:62], T.aba[:, 0:62], T.abb[:, 0:62], MAX)
+    bar()
+    for w, o in ((31, 31), (15, 16), (8, 8), (4, 4), (2, 2)):
+        tt(T.sqa[:, 0:w], T.sqa[:, 0:w], T.sqa[:, o:o + w], ADD)
+        tt(T.aba[:, 0:w], T.aba[:, 0:w], T.aba[:, o:o + w], MAX)
+        bar()
+    v.tensor_tensor(T.land[:, 0, 0:1], T.sqa[:, 0:1], T.sqa[:, 1:2], ADD).then_inc(S.mr, 1)
+    v.tensor_tensor(T.land[:, 0, 9:10], T.aba[:, 0:1], T.aba[:, 1:2], MAX).then_inc(S.mr, 1)
+
+    op(v.tensor_copy(T.land[:, 12, 1:5], T.land[:, 0, 1:5]))
+    tt(T.yb[:, :], T.dd[:, 2:130], T.ue[:, 4:132], ADD)
+    v.wait_ge(S.halo, n_halo)
+    tt(T.t4[:, :], T.hin[:, :], T.c125[:, 0:4], MUL)
+    bar()
+    tt(T.yb[:, 0:2], T.yb[:, 0:2], T.t4[:, 0:2], ADD)
+    tt(T.yb[:, 126:128], T.yb[:, 126:128], T.t4[:, 2:4], ADD)
+    bar()
+    v.tensor_tensor(T.yb[:, 0:1], T.yb[:, 0:1], T.t4[:, 1:2], ADD).then_inc(S.yr, 1)
+    v.tensor_tensor(T.yb[:, 127:128], T.yb[:, 127:128], T.t4[:, 2:3], ADD).then_inc(S.yr, 1)
+    g.scalar.wait_ge(S.yr, 2)
+    g.scalar.dma_start(T.y[:, :], T.yb[:, :]).then_inc(S.sty, 16)
+    g.scalar.wait_ge(S.sty, 16)
+
+    v.wait_ge(S.mr, 2)
+    v.wait_ge(S.arr, n_arr)
+    tt(T.dB[:, :, :], T.land[:, 0:12, 5:9], T.land[:, 1:13, 1:5], ADD)
+    bar()
+    tt(T.nB[:, :, :], T.zt[:, :, :], T.dB[:, :, :], SUB)
+    v.wait_ge(S.sent, n_sent)
+    bar()
+    tt(T.land[:, 0:12, 1:5], T.dB[:, :, :], T.nB[:, :, :], MUL)
+    tt(T.land[:, 0:12, 5:9], T.dB[:, :, :], T.nB[:, :, :], MAX)
+    bar()
+    tt(T.r6s[:, :, :], T.land[:, 0:6, 0:5], T.land[:, 6:12, 0:5], ADD)
+    tt(T.r6m[:, :, :], T.land[:, 0:6, 5:10], T.land[:, 6:12, 5:10], MAX)
+    bar()
+    tt(T.r3s[:, :, :], T.r6s[:, 0:3, :], T.r6s[:, 3:6, :], ADD)
+    tt(T.r3m[:, :, :], T.r6m[:, 0:3, :], T.r6m[:, 3:6, :], MAX)
+    bar()
+    tt(T.t5s[:, 0:5], T.r3s[:, 0, :], T.r3s[:, 1, :], ADD)
+    tt(T.t5m[:, 0:5], T.r3m[:, 0, :], T.r3m[:, 1, :], MAX)
+    bar()
+    tt(T.t5s[:, 0:5], T.t5s[:, 0:5], T.r3s[:, 2, :], ADD)
+    tt(T.t5m[:, 0:5], T.t5m[:, 0:5], T.r3m[:, 2, :], MAX)
+    bar()
+    tt(T.t2s[:, 0:2], T.t5s[:, 0:2], T.t5s[:, 2:4], ADD)
+    tt(T.t2m[:, 0:2], T.t5m[:, 0:2], T.t5m[:, 2:4], MAX)
+    bar()
+    tt(T.t2s[:, 0:1], T.t2s[:, 0:1], T.t2s[:, 1:2], ADD)
+    tt(T.t2m[:, 0:1], T.t2m[:, 0:1], T.t2m[:, 1:2], MAX)
+    bar()
+    tt(T.t2s[:, 0:1], T.t2s[:, 0:1], T.t5s[:, 4:5], ADD)
+    v.tensor_tensor(T.so[:, 1:2], T.t2m[:, 0:1], T.t5m[:, 4:5], MAX).then_inc(S.sr, 1)
+    bar()
+    v.tensor_tensor(T.so[:, 0:1], T.t2s[:, 0:1], T.sc[:, 0:1], MUL).then_inc(S.sr, 1)
+    g.sync.wait_ge(S.sr, 2)
+    g.sync.dma_start(T.s[:, :], T.so[:, :]).then_inc(S.sts, 16)
+    g.sync.wait_ge(S.sts, 16)

@@ -1,29 +1,36 @@
+import math
 from concourse.bass import DstId, RemoteDMATransfer
-from concourse.mybir import AluOpType
+from concourse.mybir import AluOpType, AxisListType, ActivationFunctionType
 
 N = 12
 F32 = "float32"
+SC = 0.125 / math.sqrt(N * 128.0)
 SCRATCH = {
-    "ue": ("sbuf", [128, 136], F32), "bb": ("sbuf", [128, 128], F32),
-    "c125": ("sbuf", [128, 132], F32), "c5": ("sbuf", [128, 128], F32),
-    "pp": ("sbuf", [128, 136], F32), "a8": ("sbuf", [128, 132], F32), "dd": ("sbuf", [128, 132], F32),
+    "ue": ("sbuf", [128, 136], F32), "bb": ("sbuf", [128, 128], F32), "b4e": ("sbuf", [128, 132], F32),
+    "pp": ("sbuf", [128, 136], F32), "nw8": ("sbuf", [128, 132], F32), "dd": ("sbuf", [128, 136], F32),
+    "sqj": ("sbuf", [128, 124], F32),
     "yb": ("sbuf", [128, 128], F32), "hin": ("sbuf", [128, 4], F32), "t4": ("sbuf", [128, 4], F32),
-    "sqa": ("sbuf", [128, 64], F32), "aba": ("sbuf", [128, 64], F32),
     "land": ("sbuf", [128, 13, 12], F32),
-    "dB": ("sbuf", [128, 12, 4], F32), "nB": ("sbuf", [128, 12, 4], F32), "zt": ("sbuf", [128, 12, 4], F32),
-    "r6s": ("sbuf", [128, 6, 5], F32), "r6m": ("sbuf", [128, 6, 5], F32),
-    "r3s": ("sbuf", [128, 3, 5], F32), "r3m": ("sbuf", [128, 3, 5], F32),
-    "t5s": ("sbuf", [128, 8], F32), "t5m": ("sbuf", [128, 8], F32),
-    "t2s": ("sbuf", [128, 4], F32), "t2m": ("sbuf", [128, 4], F32),
-    "sc": ("sbuf", [128, 4], F32), "so": ("sbuf", [128, 2], F32),
-    "Ap": ("psum", [128, 512], F32), "hbp": ("psum", [128, 512], F32), "nwp": ("psum", [128, 512], F32),
-    "ndp": ("psum", [128, 512], F32), "sqb": ("psum", [128, 512], F32), "abb": ("psum", [128, 512], F32),
+    "cat": ("sbuf", [128, 60], F32), "j48": ("sbuf", [128, 48], F32), "j12": ("sbuf", [128, 12], F32),
+    "s1": ("sbuf", [128, 4], F32), "s2": ("sbuf", [128, 4], F32), "tm": ("sbuf", [128, 4], F32),
+    "so": ("sbuf", [128, 2], F32),
+    "Ap": ("psum", [128, 512], F32), "u8p": ("psum", [128, 512], F32), "dP": ("psum", [128, 512], F32),
 }
-SEMAPHORES = ["ldu", "ldb", "v", "mr", "halo", "arr", "sent", "yr", "sr", "sty", "sts"]
+SEMAPHORES = ["ldu", "ldb", "ms", "v", "su", "sb", "dm", "mr", "own", "yp", "halo", "arr", "sent", "yr", "sty",
+              "fa", "fc", "f2", "f1", "sr", "sts"]
 
 
 def _bits(m):
     return bin(m).count("1")
+
+
+def _low(m, k):
+    out = 0
+    for i in range(m.bit_length()):
+        if k and (m >> i) & 1:
+            out |= 1 << i
+            k -= 1
+    return out
 
 
 def rank_program(g, core, T, topo):
@@ -32,8 +39,9 @@ def rank_program(g, core, T, topo):
         return
     cores = list(T.cores)
     S = T.sem
-    v = g.vector
+    v, a = g.vector, g.scalar
     ADD, SUB, MUL, MAX = AluOpType.add, AluOpType.subtract, AluOpType.mult, AluOpType.max
+    AF = ActivationFunctionType
 
     def emask(src, dst):
         m = topo.mask(src, dst)
@@ -43,13 +51,13 @@ def rank_program(g, core, T, topo):
         for c in cores:
             if topo.chip(c) != topo.chip(src):
                 off |= topo.mask(src, c)
-        return (m & ~off) or m
+        return _low((m & ~off) or m, 2)
 
     def hops(src, dst):
-        a, b = topo.chip(src), topo.chip(dst)
-        if a == b:
+        x, y = topo.chip(src), topo.chip(dst)
+        if x == y:
             return 0
-        return 1 if (topo.mates(a, b) or topo.same_plane(a, b)) else 2
+        return 1 if (topo.mates(x, y) or topo.same_plane(x, y)) else 2
 
     def did(c):
         rid, pid, _se = topo.addr(c)
@@ -59,7 +67,7 @@ def rank_program(g, core, T, topo):
     others = sorted([c for c in cores if c != core], key=lambda c: -hops(core, c))
 
     g.sync.dma_start(T.ue[:, 4:132], T.u[:, :]).then_inc(S.ldu, 16)
-    g.scalar.dma_start(T.bb[:, :], T.b[:, :]).then_inc(S.ldb, 16)
+    a.dma_start(T.bb[:, :], T.b[:, :]).then_inc(S.ldb, 16)
 
     g.wait_ge(S.ldu, 16)
     g.remote_dma_fused([
@@ -72,10 +80,11 @@ def rank_program(g, core, T, topo):
     groups = {}
     for c in others:
         groups.setdefault(emask(core, c), []).append(c)
-    g.wait_ge(S.mr, 2)
+    g.wait_ge(S.dm, 1)
+    g.wait_ge(S.mr, 3)
     g.remote_dma_fused([
         RemoteDMATransfer(dst_ids=[did(c) for c in cs], dma_engine_mask=m, remote_sem=S.arr,
-                          srcs=[T.land[:, 0, 0:10]],
+                          srcs=[T.dd[:, 124:134]],
                           dsts=[T.land[:, (rank - T.rank_of(c)) % N, 0:10] for c in cs], alu_op=0)
         for m, cs in groups.items()], local_sem=S.sent)
     n_sent += sum(_bits(m) for m in groups)
@@ -92,94 +101,76 @@ def rank_program(g, core, T, topo):
     def bar():
         v.wait_ge(S.v, cnt[0])
 
-    def tt(out, a, b, o):
-        op(v.tensor_tensor(out, a, b, o))
+    def tt(out, x, y, o):
+        op(v.tensor_tensor(out, x, y, o))
 
-    op(v.memset(T.ue[:, 0:4], 0.0))
-    op(v.memset(T.ue[:, 132:136], 0.0))
-    op(v.memset(T.c125[:, :], 0.125))
-    op(v.memset(T.c5[:, :], 0.5))
-    op(v.memset(T.hbp[:, 0:2], 0.0))
-    op(v.memset(T.hbp[:, 130:132], 0.0))
-    op(v.memset(T.zt[:, :, :], 0.0))
-    op(v.memset(T.sc[:, :], -1.0 / (N * 128)))
-    bar()
+    v.memset(T.ue[:, 0:4], 0.0).then_inc(S.ms, 1)
+    v.memset(T.ue[:, 132:136], 0.0).then_inc(S.ms, 1)
+    v.memset(T.b4e[:, 0:2], 0.0).then_inc(S.ms, 1)
+    v.memset(T.b4e[:, 130:132], 0.0).then_inc(S.ms, 1)
+
+    a.wait_ge(S.ms, 4)
+    a.wait_ge(S.ldu, 16)
+    a.activation(T.u8p[:, 0:132], T.ue[:, 2:134], AF.Copy, scale=8.0).then_inc(S.su, 1)
+    a.wait_ge(S.ldb, 16)
+    a.activation(T.b4e[:, 2:130], T.bb[:, :], AF.Copy, scale=4.0).then_inc(S.sb, 1)
+
+    v.wait_ge(S.ms, 4)
     v.wait_ge(S.ldu, 16)
     tt(T.pp[:, 0:135], T.ue[:, 0:135], T.ue[:, 1:136], ADD)
     bar()
     tt(T.Ap[:, 0:132], T.pp[:, 0:132], T.pp[:, 3:135], ADD)
-    v.wait_ge(S.ldb, 16)
-    tt(T.hbp[:, 2:130], T.bb[:, :], T.c5[:, :], MUL)
+    v.wait_ge(S.su, 1)
+    v.wait_ge(S.sb, 1)
+    tt(T.nw8[:, :], T.u8p[:, 0:132], T.b4e[:, :], SUB)
     bar()
-    tt(T.a8[:, :], T.Ap[:, 0:132], T.c125[:, :], MUL)
-    tt(T.nwp[:, 0:132], T.ue[:, 2:134], T.hbp[:, 0:132], SUB)
-    bar()
-    tt(T.dd[:, 2:130], T.a8[:, 2:130], T.nwp[:, 2:130], SUB)
-    tt(T.ndp[:, 0:124], T.nwp[:, 4:128], T.a8[:, 4:128], SUB)
-    tt(T.land[:, 0, 1:5], T.a8[:, 0:4], T.nwp[:, 0:4], SUB)
-    tt(T.land[:, 0, 5:9], T.a8[:, 128:132], T.nwp[:, 128:132], SUB)
-    bar()
-    tt(T.sqa[:, 0:62], T.dd[:, 4:66], T.ndp[:, 0:62], MUL)
-    tt(T.sqb[:, 0:62], T.dd[:, 66:128], T.ndp[:, 62:124], MUL)
-    tt(T.aba[:, 0:62], T.dd[:, 4:66], T.ndp[:, 0:62], MAX)
-    tt(T.abb[:, 0:62], T.dd[:, 66:128], T.ndp[:, 62:124], MAX)
-    bar()
-    tt(T.sqa[:, 0:62], T.sqa[:, 0:62], T.sqb[:, 0:62], ADD)
-    tt(T.aba[:, 0:62], T.aba[:, 0:62], T.abb[:, 0:62], MAX)
-    bar()
-    for w, o in ((31, 31), (15, 16), (8, 8), (4, 4), (2, 2)):
-        tt(T.sqa[:, 0:w], T.sqa[:, 0:w], T.sqa[:, o:o + w], ADD)
-        tt(T.aba[:, 0:w], T.aba[:, 0:w], T.aba[:, o:o + w], MAX)
-        bar()
-    v.tensor_tensor(T.land[:, 0, 0:1], T.sqa[:, 0:1], T.sqa[:, 1:2], ADD).then_inc(S.mr, 1)
-    v.tensor_tensor(T.land[:, 0, 9:10], T.aba[:, 0:1], T.aba[:, 1:2], MAX).then_inc(S.mr, 1)
+    v.tensor_tensor(T.dd[:, 0:128], T.Ap[:, 4:132], T.nw8[:, 4:132], SUB).then_inc(S.dm, 1)
+    v.tensor_tensor(T.dd[:, 128:132], T.Ap[:, 0:4], T.nw8[:, 0:4], SUB).then_inc(S.mr, 1)
+    v.wait_ge(S.dm, 1)
+    v.tensor_reduce(T.dd[:, 133:134], T.dd[:, 0:124], AxisListType.X, MAX,
+                    apply_absolute_value=True).then_inc(S.mr, 1)
+    a.wait_ge(S.dm, 1)
+    a.activation(T.sqj[:, :], T.dd[:, 0:124], AF.Square, scale=SC, accum_out=T.dd[:, 132:133]).then_inc(S.mr, 1)
 
-    op(v.tensor_copy(T.land[:, 12, 1:5], T.land[:, 0, 1:5]))
-    tt(T.yb[:, :], T.dd[:, 2:130], T.ue[:, 4:132], ADD)
+    v.wait_ge(S.mr, 3)
+    v.tensor_copy(T.land[:, 0, 0:10], T.dd[:, 124:134]).then_inc(S.own, 1)
+    v.tensor_copy(T.land[:, 12, 4:8], T.dd[:, 128:132]).then_inc(S.own, 1)
+    a.wait_ge(S.mr, 3)
+    a.activation(T.dP[:, 0:132], T.dd[:, 0:132], AF.Copy, scale=0.125).then_inc(S.yp, 1)
+    v.wait_ge(S.yp, 1)
+    tt(T.yb[:, 2:128], T.dP[:, 0:126], T.ue[:, 6:132], ADD)
+    tt(T.yb[:, 0:2], T.dP[:, 130:132], T.ue[:, 4:6], ADD)
     v.wait_ge(S.halo, n_halo)
-    tt(T.t4[:, :], T.hin[:, :], T.c125[:, 0:4], MUL)
+    op(v.tensor_scalar(T.t4[:, :], T.hin[:, :], 0.125, None, MUL))
     bar()
     tt(T.yb[:, 0:2], T.yb[:, 0:2], T.t4[:, 0:2], ADD)
     tt(T.yb[:, 126:128], T.yb[:, 126:128], T.t4[:, 2:4], ADD)
     bar()
     v.tensor_tensor(T.yb[:, 0:1], T.yb[:, 0:1], T.t4[:, 1:2], ADD).then_inc(S.yr, 1)
     v.tensor_tensor(T.yb[:, 127:128], T.yb[:, 127:128], T.t4[:, 2:3], ADD).then_inc(S.yr, 1)
-    g.scalar.wait_ge(S.yr, 2)
-    g.scalar.dma_start(T.y[:, :], T.yb[:, :]).then_inc(S.sty, 16)
-    g.scalar.wait_ge(S.sty, 16)
+    a.wait_ge(S.yr, 2)
+    a.dma_start(T.y[:, :], T.yb[:, :]).then_inc(S.sty, 16)
 
-    v.wait_ge(S.mr, 2)
+    v.wait_ge(S.own, 2)
     v.wait_ge(S.arr, n_arr)
-    tt(T.dB[:, :, :], T.land[:, 0:12, 5:9], T.land[:, 1:13, 1:5], ADD)
+    for i in range(4):
+        v.tensor_tensor(T.cat[:, 12 * i:12 * i + 12], T.land[:, 0:12, i], T.land[:, 1:13, 4 + i],
+                        ADD).then_inc(S.fa, 1)
+    a.wait_ge(S.own, 2)
+    a.wait_ge(S.arr, n_arr)
+    a.activation(T.cat[:, 48:60], T.land[:, 0:12, 9], AF.Copy).then_inc(S.fc, 1)
+    a.activation(T.j12[:, :], T.land[:, 0:12, 8], AF.Copy, accum_out=T.s2[:, 0:1]).then_inc(S.f2, 1)
+    a.wait_ge(S.fa, 4)
+    a.activation(T.j48[:, :], T.cat[:, 0:48], AF.Square, scale=SC, accum_out=T.s1[:, 0:1]).then_inc(S.f1, 1)
+    a.wait_ge(S.f2, 1)
+    a.wait_ge(S.f1, 1)
+    a.activation(T.so[:, 0:1], T.s1[:, 0:1], AF.Identity, bias=T.s2[:, 0:1], scale=1.0).then_inc(S.sr, 1)
+    v.wait_ge(S.fa, 4)
+    v.wait_ge(S.fc, 1)
+    op(v.tensor_reduce(T.tm[:, 0:1], T.cat[:, 0:60], AxisListType.X, MAX, apply_absolute_value=True))
     bar()
-    tt(T.nB[:, :, :], T.zt[:, :, :], T.dB[:, :, :], SUB)
-    v.wait_ge(S.sent, n_sent)
-    bar()
-    tt(T.land[:, 0:12, 1:5], T.dB[:, :, :], T.nB[:, :, :], MUL)
-    tt(T.land[:, 0:12, 5:9], T.dB[:, :, :], T.nB[:, :, :], MAX)
-    bar()
-    tt(T.r6s[:, :, :], T.land[:, 0:6, 0:5], T.land[:, 6:12, 0:5], ADD)
-    tt(T.r6m[:, :, :], T.land[:, 0:6, 5:10], T.land[:, 6:12, 5:10], MAX)
-    bar()
-    tt(T.r3s[:, :, :], T.r6s[:, 0:3, :], T.r6s[:, 3:6, :], ADD)
-    tt(T.r3m[:, :, :], T.r6m[:, 0:3, :], T.r6m[:, 3:6, :], MAX)
-    bar()
-    tt(T.t5s[:, 0:5], T.r3s[:, 0, :], T.r3s[:, 1, :], ADD)
-    tt(T.t5m[:, 0:5], T.r3m[:, 0, :], T.r3m[:, 1, :], MAX)
-    bar()
-    tt(T.t5s[:, 0:5], T.t5s[:, 0:5], T.r3s[:, 2, :], ADD)
-    tt(T.t5m[:, 0:5], T.t5m[:, 0:5], T.r3m[:, 2, :], MAX)
-    bar()
-    tt(T.t2s[:, 0:2], T.t5s[:, 0:2], T.t5s[:, 2:4], ADD)
-    tt(T.t2m[:, 0:2], T.t5m[:, 0:2], T.t5m[:, 2:4], MAX)
-    bar()
-    tt(T.t2s[:, 0:1], T.t2s[:, 0:1], T.t2s[:, 1:2], ADD)
-    tt(T.t2m[:, 0:1], T.t2m[:, 0:1], T.t2m[:, 1:2], MAX)
-    bar()
-    tt(T.t2s[:, 0:1], T.t2s[:, 0:1], T.t5s[:, 4:5], ADD)
-    v.tensor_tensor(T.so[:, 1:2], T.t2m[:, 0:1], T.t5m[:, 4:5], MAX).then_inc(S.sr, 1)
-    bar()
-    v.tensor_tensor(T.so[:, 0:1], T.t2s[:, 0:1], T.sc[:, 0:1], MUL).then_inc(S.sr, 1)
+    v.tensor_scalar(T.so[:, 1:2], T.tm[:, 0:1], 0.125, None, MUL).then_inc(S.sr, 1)
     g.sync.wait_ge(S.sr, 2)
     g.sync.dma_start(T.s[:, :], T.so[:, :]).then_inc(S.sts, 16)
     g.sync.wait_ge(S.sts, 16)
+    a.wait_ge(S.sty, 16)

@@ -4,20 +4,18 @@ from concourse.mybir import AluOpType, AxisListType, ActivationFunctionType
 
 N = 12
 F32 = "float32"
-SC = 0.125 / math.sqrt(N * 128.0)
 SCRATCH = {
-    "ue": ("sbuf", [128, 136], F32), "bb": ("sbuf", [128, 128], F32), "b4e": ("sbuf", [128, 132], F32),
-    "pp": ("sbuf", [128, 136], F32), "nw8": ("sbuf", [128, 132], F32), "dd": ("sbuf", [128, 136], F32),
-    "sqj": ("sbuf", [128, 124], F32),
+    "ue": ("sbuf", [128, 144], F32), "bb": ("sbuf", [128, 128], F32),
+    "w5": ("sbuf", [128, 132], F32), "ff": ("sbuf", [128, 132], F32), "dd": ("sbuf", [128, 132], F32),
+    "sqj": ("sbuf", [128, 132], F32),
     "yb": ("sbuf", [128, 128], F32), "hin": ("sbuf", [128, 4], F32), "t4": ("sbuf", [128, 4], F32),
     "land": ("sbuf", [128, 13, 12], F32),
-    "cat": ("sbuf", [128, 60], F32), "j48": ("sbuf", [128, 48], F32), "j12": ("sbuf", [128, 12], F32),
-    "s1": ("sbuf", [128, 4], F32), "s2": ("sbuf", [128, 4], F32), "tm": ("sbuf", [128, 4], F32),
+    "cat": ("sbuf", [128, 60], F32), "cat2": ("sbuf", [128, 60], F32), "j60": ("sbuf", [128, 60], F32),
     "so": ("sbuf", [128, 2], F32),
-    "Ap": ("psum", [128, 512], F32), "u8p": ("psum", [128, 512], F32), "dP": ("psum", [128, 512], F32),
+    "u9p": ("psum", [128, 512], F32), "b4p": ("psum", [128, 512], F32), "dP": ("psum", [128, 512], F32),
 }
 SEMAPHORES = ["ldu", "ldb", "ms", "v", "su", "sb", "dm", "mr", "own", "yp", "halo", "arr", "sent", "yr", "sty",
-              "fa", "fc", "f2", "f1", "sr", "sts"]
+              "fp", "fq", "fc", "f2", "sr", "sts"]
 
 
 def _bits(m):
@@ -53,41 +51,82 @@ def rank_program(g, core, T, topo):
                 off |= topo.mask(src, c)
         return _low((m & ~off) or m, 2)
 
-    def hops(src, dst):
-        x, y = topo.chip(src), topo.chip(dst)
-        if x == y:
-            return 0
-        return 1 if (topo.mates(x, y) or topo.same_plane(x, y)) else 2
-
     def did(c):
         rid, pid, _se = topo.addr(c)
         return DstId(rid=rid, pnc=pid)
 
     left, right = cores[(rank - 1) % N], cores[(rank + 1) % N]
-    others = sorted([c for c in cores if c != core], key=lambda c: -hops(core, c))
 
-    g.sync.dma_start(T.ue[:, 4:132], T.u[:, :]).then_inc(S.ldu, 16)
+    chips = []
+    for c in cores:
+        if topo.chip(c) not in chips:
+            chips.append(topo.chip(c))
+    members = {ch: [c for c in cores if topo.chip(c) == ch] for ch in chips}
+
+    def far(x, y):
+        return 0 if (topo.mates(x, y) or topo.same_plane(x, y)) else 1
+
+    def matchings(rem):
+        if not rem:
+            return [[]]
+        out = []
+        for y in rem[1:]:
+            rest = [z for z in rem[1:] if z != y]
+            out += [[(rem[0], y)] + m for m in matchings(rest)]
+        return out
+
+    allm = matchings(chips)
+
+    def plans(start, used, chosen):
+        if len(chosen) == len(chips) - 1:
+            return [chosen]
+        out = []
+        for i in range(start, len(allm)):
+            if not any(p in used for p in allm[i]):
+                out += plans(i + 1, used | set(allm[i]), chosen + [allm[i]])
+        return out
+
+    def weight(m):
+        return sum(far(x, y) for x, y in m)
+
+    best = None
+    for f in plans(0, set(), []):
+        f = sorted(f, key=lambda m: -weight(m))
+        key = [weight(m) for m in reversed(f)]
+        if best is None or key < best[0]:
+            best = (key, f)
+    mychip = topo.chip(core)
+    pos = members[mychip].index(core)
+    near = [c for c in members[mychip] if c != core]
+    away = []
+    for m in best[1]:
+        for x, y in m:
+            if mychip in (x, y):
+                mem = members[y if x == mychip else x]
+                away += [mem[(pos + j) % len(mem)] for j in range(len(mem))]
+    others = near + away
+
+    g.sync.dma_start(T.ue[:, 8:136], T.u[:, :]).then_inc(S.ldu, 16)
     a.dma_start(T.bb[:, :], T.b[:, :]).then_inc(S.ldb, 16)
 
+    edge = {left: (T.ue[:, 8:10], T.hin[:, 2:4]), right: (T.ue[:, 134:136], T.hin[:, 0:2])}
+    n_sent = 0
     g.wait_ge(S.ldu, 16)
-    g.remote_dma_fused([
-        RemoteDMATransfer(dst_ids=[did(left)], dma_engine_mask=emask(core, left), remote_sem=S.halo,
-                          srcs=[T.ue[:, 4:6]], dsts=[T.hin[:, 2:4]], alu_op=0),
-        RemoteDMATransfer(dst_ids=[did(right)], dma_engine_mask=emask(core, right), remote_sem=S.halo,
-                          srcs=[T.ue[:, 130:132]], dsts=[T.hin[:, 0:2]], alu_op=0),
-    ], local_sem=S.sent)
-    n_sent = _bits(emask(core, left)) + _bits(emask(core, right))
-    groups = {}
-    for c in others:
-        groups.setdefault(emask(core, c), []).append(c)
-    g.wait_ge(S.dm, 1)
-    g.wait_ge(S.mr, 3)
-    g.remote_dma_fused([
-        RemoteDMATransfer(dst_ids=[did(c) for c in cs], dma_engine_mask=m, remote_sem=S.arr,
-                          srcs=[T.dd[:, 124:134]],
-                          dsts=[T.land[:, (rank - T.rank_of(c)) % N, 0:10] for c in cs], alu_op=0)
-        for m, cs in groups.items()], local_sem=S.sent)
-    n_sent += sum(_bits(m) for m in groups)
+    for c in sorted(edge, key=lambda c: topo.chip(c) != mychip):
+        g.remote_dma_fused([RemoteDMATransfer(dst_ids=[did(c)], dma_engine_mask=emask(core, c), remote_sem=S.halo,
+                                              srcs=[edge[c][0]], dsts=[edge[c][1]], alu_op=0)], local_sem=S.sent)
+        n_sent += _bits(emask(core, c))
+    g.wait_ge(S.mr, 4)
+    for cs in (away, near):
+        groups = {}
+        for c in cs:
+            groups.setdefault(emask(core, c), []).append(c)
+        g.remote_dma_fused([
+            RemoteDMATransfer(dst_ids=[did(c) for c in gs], dma_engine_mask=m, remote_sem=S.arr,
+                              srcs=[T.land[:, 0, 0:10]],
+                              dsts=[T.land[:, (rank - T.rank_of(c)) % N, 0:10] for c in gs], alu_op=0)
+            for m, gs in groups.items()], local_sem=S.sent)
+        n_sent += sum(_bits(m) for m in groups)
     g.wait_ge(S.sent, n_sent)
     n_halo = _bits(emask(left, core)) + _bits(emask(right, core))
     n_arr = sum(_bits(emask(c, core)) for c in others)
@@ -104,42 +143,40 @@ def rank_program(g, core, T, topo):
     def tt(out, x, y, o):
         op(v.tensor_tensor(out, x, y, o))
 
-    v.memset(T.ue[:, 0:4], 0.0).then_inc(S.ms, 1)
-    v.memset(T.ue[:, 132:136], 0.0).then_inc(S.ms, 1)
-    v.memset(T.b4e[:, 0:2], 0.0).then_inc(S.ms, 1)
-    v.memset(T.b4e[:, 130:132], 0.0).then_inc(S.ms, 1)
+    v.memset(T.ue[:, 0:8], 0.0).then_inc(S.ms, 1)
+    v.memset(T.ue[:, 136:144], 0.0).then_inc(S.ms, 1)
+    v.memset(T.b4p[:, 0:2], 0.0).then_inc(S.ms, 1)
+    v.memset(T.b4p[:, 130:132], 0.0).then_inc(S.ms, 1)
 
     a.wait_ge(S.ms, 4)
     a.wait_ge(S.ldu, 16)
-    a.activation(T.u8p[:, 0:132], T.ue[:, 2:134], AF.Copy, scale=8.0).then_inc(S.su, 1)
+    a.activation(T.u9p[:, 0:132], T.ue[:, 6:138], AF.Copy, scale=9.0).then_inc(S.su, 1)
     a.wait_ge(S.ldb, 16)
-    a.activation(T.b4e[:, 2:130], T.bb[:, :], AF.Copy, scale=4.0).then_inc(S.sb, 1)
+    a.activation(T.b4p[:, 2:130], T.bb[:, :], AF.Copy, scale=4.0).then_inc(S.sb, 1)
 
     v.wait_ge(S.ms, 4)
     v.wait_ge(S.ldu, 16)
-    tt(T.pp[:, 0:135], T.ue[:, 0:135], T.ue[:, 1:136], ADD)
-    bar()
-    tt(T.Ap[:, 0:132], T.pp[:, 0:132], T.pp[:, 3:135], ADD)
+    op(v.tensor_tensor_scan(T.w5[:, :], T.ue[:, 8:140], T.ue[:, 3:135], 0.0, ADD, SUB))
     v.wait_ge(S.su, 1)
-    v.wait_ge(S.sb, 1)
-    tt(T.nw8[:, :], T.u8p[:, 0:132], T.b4e[:, :], SUB)
     bar()
-    v.tensor_tensor(T.dd[:, 0:128], T.Ap[:, 4:132], T.nw8[:, 4:132], SUB).then_inc(S.dm, 1)
-    v.tensor_tensor(T.dd[:, 128:132], T.Ap[:, 0:4], T.nw8[:, 0:4], SUB).then_inc(S.mr, 1)
-    v.wait_ge(S.dm, 1)
-    v.tensor_reduce(T.dd[:, 133:134], T.dd[:, 0:124], AxisListType.X, MAX,
-                    apply_absolute_value=True).then_inc(S.mr, 1)
-    a.wait_ge(S.dm, 1)
-    a.activation(T.sqj[:, :], T.dd[:, 0:124], AF.Square, scale=SC, accum_out=T.dd[:, 132:133]).then_inc(S.mr, 1)
+    tt(T.ff[:, :], T.w5[:, :], T.u9p[:, 0:132], SUB)
+    v.wait_ge(S.sb, 1)
+    bar()
+    v.tensor_tensor(T.dd[:, :], T.ff[:, :], T.b4p[:, 0:132], ADD).then_inc(S.dm, 1)
 
-    v.wait_ge(S.mr, 3)
-    v.tensor_copy(T.land[:, 0, 0:10], T.dd[:, 124:134]).then_inc(S.own, 1)
-    v.tensor_copy(T.land[:, 12, 4:8], T.dd[:, 128:132]).then_inc(S.own, 1)
-    a.wait_ge(S.mr, 3)
-    a.activation(T.dP[:, 0:132], T.dd[:, 0:132], AF.Copy, scale=0.125).then_inc(S.yp, 1)
+    v.wait_ge(S.dm, 1)
+    v.tensor_reduce(T.land[:, 0, 9:10], T.dd[:, 4:128], AxisListType.X, MAX,
+                    apply_absolute_value=True).then_inc(S.mr, 1)
+    v.tensor_scalar(T.land[:, 0, 0:4], T.dd[:, 128:132], 0.125, None, MUL).then_inc(S.mr, 1)
+    a.wait_ge(S.dm, 1)
+    a.activation(T.sqj[:, :], T.dd[:, :], AF.Square, scale=0.125, accum_out=T.land[:, 0, 8:9]).then_inc(S.mr, 1)
+    a.activation(T.land[:, 0, 4:8], T.dd[:, 0:4], AF.Copy, scale=0.125).then_inc(S.mr, 1)
+
+    a.activation(T.dP[:, 0:128], T.dd[:, 2:130], AF.Copy, scale=0.125).then_inc(S.yp, 1)
+    v.wait_ge(S.mr, 4)
+    v.tensor_copy(T.land[:, 12, 4:8], T.land[:, 0, 4:8]).then_inc(S.own, 1)
     v.wait_ge(S.yp, 1)
-    tt(T.yb[:, 2:128], T.dP[:, 0:126], T.ue[:, 6:132], ADD)
-    tt(T.yb[:, 0:2], T.dP[:, 130:132], T.ue[:, 4:6], ADD)
+    tt(T.yb[:, :], T.dP[:, 0:128], T.ue[:, 8:136], ADD)
     v.wait_ge(S.halo, n_halo)
     op(v.tensor_scalar(T.t4[:, :], T.hin[:, :], 0.125, None, MUL))
     bar()
@@ -148,29 +185,25 @@ def rank_program(g, core, T, topo):
     bar()
     v.tensor_tensor(T.yb[:, 0:1], T.yb[:, 0:1], T.t4[:, 1:2], ADD).then_inc(S.yr, 1)
     v.tensor_tensor(T.yb[:, 127:128], T.yb[:, 127:128], T.t4[:, 2:3], ADD).then_inc(S.yr, 1)
-    a.wait_ge(S.yr, 2)
-    a.dma_start(T.y[:, :], T.yb[:, :]).then_inc(S.sty, 16)
+    g.sync.wait_ge(S.yr, 2)
+    g.sync.dma_start(T.y[:, :], T.yb[:, :]).then_inc(S.sty, 16)
 
-    v.wait_ge(S.own, 2)
+    v.wait_ge(S.own, 1)
     v.wait_ge(S.arr, n_arr)
-    for i in range(4):
-        v.tensor_tensor(T.cat[:, 12 * i:12 * i + 12], T.land[:, 0:12, i], T.land[:, 1:13, 4 + i],
-                        ADD).then_inc(S.fa, 1)
-    a.wait_ge(S.own, 2)
+    v.tensor_tensor(T.cat2[:, 0:48], T.land[:, 0:12, 0:4], T.land[:, 1:13, 4:8], MUL).then_inc(S.fp, 1)
+    v.tensor_tensor(T.cat[:, 0:48], T.land[:, 0:12, 0:4], T.land[:, 1:13, 4:8], ADD).then_inc(S.fq, 1)
+    a.wait_ge(S.mr, 4)
     a.wait_ge(S.arr, n_arr)
-    a.activation(T.cat[:, 48:60], T.land[:, 0:12, 9], AF.Copy).then_inc(S.fc, 1)
-    a.activation(T.j12[:, :], T.land[:, 0:12, 8], AF.Copy, accum_out=T.s2[:, 0:1]).then_inc(S.f2, 1)
-    a.wait_ge(S.fa, 4)
-    a.activation(T.j48[:, :], T.cat[:, 0:48], AF.Square, scale=SC, accum_out=T.s1[:, 0:1]).then_inc(S.f1, 1)
+    a.activation(T.cat2[:, 48:60], T.land[:, 0:12, 8], AF.Copy, scale=0.5).then_inc(S.f2, 1)
+    a.activation(T.cat[:, 48:60], T.land[:, 0:12, 9], AF.Copy, scale=0.125).then_inc(S.fc, 1)
     a.wait_ge(S.f2, 1)
-    a.wait_ge(S.f1, 1)
-    a.activation(T.so[:, 0:1], T.s1[:, 0:1], AF.Identity, bias=T.s2[:, 0:1], scale=1.0).then_inc(S.sr, 1)
-    v.wait_ge(S.fa, 4)
+    a.wait_ge(S.fp, 1)
+    a.activation(T.j60[:, :], T.cat2[:, :], AF.Copy, scale=2.0 / (N * 128.0),
+                 accum_out=T.so[:, 0:1]).then_inc(S.sr, 1)
+    v.wait_ge(S.fq, 1)
     v.wait_ge(S.fc, 1)
-    op(v.tensor_reduce(T.tm[:, 0:1], T.cat[:, 0:60], AxisListType.X, MAX, apply_absolute_value=True))
-    bar()
-    v.tensor_scalar(T.so[:, 1:2], T.tm[:, 0:1], 0.125, None, MUL).then_inc(S.sr, 1)
+    v.tensor_reduce(T.so[:, 1:2], T.cat[:, :], AxisListType.X, MAX, apply_absolute_value=True).then_inc(S.sr, 1)
     g.sync.wait_ge(S.sr, 2)
     g.sync.dma_start(T.s[:, :], T.so[:, :]).then_inc(S.sts, 16)
     g.sync.wait_ge(S.sts, 16)
-    a.wait_ge(S.sty, 16)
+    g.sync.wait_ge(S.sty, 16)

import math
from concourse.bass import DstId, RemoteDMATransfer
from concourse.mybir import AluOpType, AxisListType, ActivationFunctionType

N = 12
F32 = "float32"
SCRATCH = {
    "ue": ("sbuf", [128, 144], F32), "bb": ("sbuf", [128, 128], F32),
    "w5": ("sbuf", [128, 132], F32), "ff": ("sbuf", [128, 132], F32), "dd": ("sbuf", [128, 132], F32),
    "sqj": ("sbuf", [128, 132], F32),
    "yb": ("sbuf", [128, 128], F32), "hin": ("sbuf", [128, 4], F32), "t4": ("sbuf", [128, 4], F32),
    "land": ("sbuf", [128, 13, 12], F32),
    "cat": ("sbuf", [128, 60], F32), "cat2": ("sbuf", [128, 60], F32), "j60": ("sbuf", [128, 60], F32),
    "so": ("sbuf", [128, 2], F32),
    "u9p": ("psum", [128, 512], F32), "b4p": ("psum", [128, 512], F32), "dP": ("psum", [128, 512], F32),
}
SEMAPHORES = ["ldu", "ldb", "ms", "v", "su", "sb", "dm", "mr", "own", "yp", "halo", "arr", "sent", "yr", "sty",
              "fp", "fq", "fc", "f2", "sr", "sts"]


def _bits(m):
    return bin(m).count("1")


def _low(m, k):
    out = 0
    for i in range(m.bit_length()):
        if k and (m >> i) & 1:
            out |= 1 << i
            k -= 1
    return out


def rank_program(g, core, T, topo):
    rank = T.rank_of(core)
    if rank is None:
        return
    cores = list(T.cores)
    S = T.sem
    v, a = g.vector, g.scalar
    ADD, SUB, MUL, MAX = AluOpType.add, AluOpType.subtract, AluOpType.mult, AluOpType.max
    AF = ActivationFunctionType

    def emask(src, dst):
        m = topo.mask(src, dst)
        if topo.chip(src) != topo.chip(dst):
            return m
        off = 0
        for c in cores:
            if topo.chip(c) != topo.chip(src):
                off |= topo.mask(src, c)
        return _low((m & ~off) or m, 2)

    def did(c):
        rid, pid, _se = topo.addr(c)
        return DstId(rid=rid, pnc=pid)

    left, right = cores[(rank - 1) % N], cores[(rank + 1) % N]

    chips = []
    for c in cores:
        if topo.chip(c) not in chips:
            chips.append(topo.chip(c))
    members = {ch: [c for c in cores if topo.chip(c) == ch] for ch in chips}

    def far(x, y):
        return 0 if (topo.mates(x, y) or topo.same_plane(x, y)) else 1

    def matchings(rem):
        if not rem:
            return [[]]
        out = []
        for y in rem[1:]:
            rest = [z for z in rem[1:] if z != y]
            out += [[(rem[0], y)] + m for m in matchings(rest)]
        return out

    allm = matchings(chips)

    def plans(start, used, chosen):
        if len(chosen) == len(chips) - 1:
            return [chosen]
        out = []
        for i in range(start, len(allm)):
            if not any(p in used for p in allm[i]):
                out += plans(i + 1, used | set(allm[i]), chosen + [allm[i]])
        return out

    def weight(m):
        return sum(far(x, y) for x, y in m)

    best = None
    for f in plans(0, set(), []):
        f = sorted(f, key=lambda m: -weight(m))
        key = [weight(m) for m in reversed(f)]
        if best is None or key < best[0]:
            best = (key, f)
    mychip = topo.chip(core)
    pos = members[mychip].index(core)
    near = [c for c in members[mychip] if c != core]
    away = []
    for m in best[1]:
        for x, y in m:
            if mychip in (x, y):
                mem = members[y if x == mychip else x]
                away += [mem[(pos + j) % len(mem)] for j in range(len(mem))]
    others = near + away

    g.sync.dma_start(T.ue[:, 8:136], T.u[:, :]).then_inc(S.ldu, 16)
    a.dma_start(T.bb[:, :], T.b[:, :]).then_inc(S.ldb, 16)

    edge = {left: (T.ue[:, 8:10], T.hin[:, 2:4]), right: (T.ue[:, 134:136], T.hin[:, 0:2])}
    n_sent = 0
    g.wait_ge(S.ldu, 16)
    for c in sorted(edge, key=lambda c: topo.chip(c) != mychip):
        g.remote_dma_fused([RemoteDMATransfer(dst_ids=[did(c)], dma_engine_mask=emask(core, c), remote_sem=S.halo,
                                              srcs=[edge[c][0]], dsts=[edge[c][1]], alu_op=0)], local_sem=S.sent)
        n_sent += _bits(emask(core, c))
    g.wait_ge(S.mr, 4)
    for cs in (away, near):
        groups = {}
        for c in cs:
            groups.setdefault(emask(core, c), []).append(c)
        g.remote_dma_fused([
            RemoteDMATransfer(dst_ids=[did(c) for c in gs], dma_engine_mask=m, remote_sem=S.arr,
                              srcs=[T.land[:, 0, 0:10]],
                              dsts=[T.land[:, (rank - T.rank_of(c)) % N, 0:10] for c in gs], alu_op=0)
            for m, gs in groups.items()], local_sem=S.sent)
        n_sent += sum(_bits(m) for m in groups)
    g.wait_ge(S.sent, n_sent)
    n_halo = _bits(emask(left, core)) + _bits(emask(right, core))
    n_arr = sum(_bits(emask(c, core)) for c in others)

    cnt = [0]

    def op(ins):
        ins.then_inc(S.v, 1)
        cnt[0] += 1

    def bar():
        v.wait_ge(S.v, cnt[0])

    def tt(out, x, y, o):
        op(v.tensor_tensor(out, x, y, o))

    v.memset(T.ue[:, 0:8], 0.0).then_inc(S.ms, 1)
    v.memset(T.ue[:, 136:144], 0.0).then_inc(S.ms, 1)
    v.memset(T.b4p[:, 0:2], 0.0).then_inc(S.ms, 1)
    v.memset(T.b4p[:, 130:132], 0.0).then_inc(S.ms, 1)

    a.wait_ge(S.ms, 4)
    a.wait_ge(S.ldu, 16)
    a.activation(T.u9p[:, 0:132], T.ue[:, 6:138], AF.Copy, scale=9.0).then_inc(S.su, 1)
    a.wait_ge(S.ldb, 16)
    a.activation(T.b4p[:, 2:130], T.bb[:, :], AF.Copy, scale=4.0).then_inc(S.sb, 1)

    v.wait_ge(S.ms, 4)
    v.wait_ge(S.ldu, 16)
    op(v.tensor_tensor_scan(T.w5[:, :], T.ue[:, 8:140], T.ue[:, 3:135], 0.0, ADD, SUB))
    v.wait_ge(S.su, 1)
    bar()
    tt(T.ff[:, :], T.w5[:, :], T.u9p[:, 0:132], SUB)
    v.wait_ge(S.sb, 1)
    bar()
    v.tensor_tensor(T.dd[:, :], T.ff[:, :], T.b4p[:, 0:132], ADD).then_inc(S.dm, 1)

    v.wait_ge(S.dm, 1)
    v.tensor_reduce(T.land[:, 0, 9:10], T.dd[:, 4:128], AxisListType.X, MAX,
                    apply_absolute_value=True).then_inc(S.mr, 1)
    v.tensor_scalar(T.land[:, 0, 0:4], T.dd[:, 128:132], 0.125, None, MUL).then_inc(S.mr, 1)
    a.wait_ge(S.dm, 1)
    a.activation(T.sqj[:, :], T.dd[:, :], AF.Square, scale=0.125, accum_out=T.land[:, 0, 8:9]).then_inc(S.mr, 1)
    a.activation(T.land[:, 0, 4:8], T.dd[:, 0:4], AF.Copy, scale=0.125).then_inc(S.mr, 1)

    a.activation(T.dP[:, 0:128], T.dd[:, 2:130], AF.Copy, scale=0.125).then_inc(S.yp, 1)
    v.wait_ge(S.mr, 4)
    v.tensor_copy(T.land[:, 12, 4:8], T.land[:, 0, 4:8]).then_inc(S.own, 1)
    v.wait_ge(S.yp, 1)
    tt(T.yb[:, :], T.dP[:, 0:128], T.ue[:, 8:136], ADD)
    v.wait_ge(S.halo, n_halo)
    op(v.tensor_scalar(T.t4[:, :], T.hin[:, :], 0.125, None, MUL))
    bar()
    tt(T.yb[:, 0:2], T.yb[:, 0:2], T.t4[:, 0:2], ADD)
    tt(T.yb[:, 126:128], T.yb[:, 126:128], T.t4[:, 2:4], ADD)
    bar()
    v.tensor_tensor(T.yb[:, 0:1], T.yb[:, 0:1], T.t4[:, 1:2], ADD).then_inc(S.yr, 1)
    v.tensor_tensor(T.yb[:, 127:128], T.yb[:, 127:128], T.t4[:, 2:3], ADD).then_inc(S.yr, 1)
    g.sync.wait_ge(S.yr, 2)
    g.sync.dma_start(T.y[:, :], T.yb[:, :]).then_inc(S.sty, 16)

    v.wait_ge(S.own, 1)
    v.wait_ge(S.arr, n_arr)
    v.tensor_tensor(T.cat2[:, 0:48], T.land[:, 0:12, 0:4], T.land[:, 1:13, 4:8], MUL).then_inc(S.fp, 1)
    v.tensor_tensor(T.cat[:, 0:48], T.land[:, 0:12, 0:4], T.land[:, 1:13, 4:8], ADD).then_inc(S.fq, 1)
    a.wait_ge(S.mr, 4)
    a.wait_ge(S.arr, n_arr)
    a.activation(T.cat2[:, 48:60], T.land[:, 0:12, 8], AF.Copy, scale=0.5).then_inc(S.f2, 1)
    a.activation(T.cat[:, 48:60], T.land[:, 0:12, 9], AF.Copy, scale=0.125).then_inc(S.fc, 1)
    a.wait_ge(S.f2, 1)
    a.wait_ge(S.fp, 1)
    a.activation(T.j60[:, :], T.cat2[:, :], AF.Copy, scale=2.0 / (N * 128.0),
                 accum_out=T.so[:, 0:1]).then_inc(S.sr, 1)
    v.wait_ge(S.fq, 1)
    v.wait_ge(S.fc, 1)
    v.tensor_reduce(T.so[:, 1:2], T.cat[:, :], AxisListType.X, MAX, apply_absolute_value=True).then_inc(S.sr, 1)
    g.sync.wait_ge(S.sr, 2)
    g.sync.dma_start(T.s[:, :], T.so[:, :]).then_inc(S.sts, 16)
    g.sync.wait_ge(S.sts, 16)
    g.sync.wait_ge(S.sty, 16)
